import numpy as np
import ml_dtypes


def mxq(x, axis, fmt="e4m3"):
    dtype, down = {"e4m3": (ml_dtypes.float8_e4m3fn, 7), "e5m2": (ml_dtypes.float8_e5m2, 14)}[fmt]
    v = np.moveaxis(np.asarray(x, np.float32).astype(ml_dtypes.bfloat16).astype(np.float64), axis, -1)
    blocks = v.reshape(v.shape[:-1] + (-1, 32))
    amax = np.abs(blocks).max(-1, keepdims=True)
    byte = np.maximum(np.where(amax > 0, np.frexp(amax)[1] - 1 + 127, 0) - down, 1)
    scale = np.exp2(byte - 127.0)
    codes = (blocks / scale).astype(np.float32).astype(dtype).astype(np.float64)
    return np.moveaxis((codes * scale).reshape(v.shape), -1, axis)


WIDE = False


def mx_kscale(k):
    if not WIDE:
        return np.ones(k)
    levels = np.array([10, -10, 5, -5, 0])
    if k % 512:
        return np.exp2(np.random.permutation(np.resize(levels, k // 32))).repeat(32)
    a = np.empty((k // 512, 16))
    for p in range(k // 512):
        a[p, :8] = np.random.permutation(np.resize(levels, 8))
        for g in range(8):
            far = levels[np.abs(levels - a[p, g]) >= 10]
            a[p, g + 8] = far[np.random.randint(len(far))]
    return np.exp2(a.ravel()).repeat(32)


def f64(x):
    return np.asarray(x).astype(np.float64)


def striped(idx):
    return np.tile(np.asarray(idx).reshape(-1, 16).T, (8, 1)).astype(np.uint16)


def unstriped(offs):
    return offs[:16].T.reshape(-1).astype(np.int64)


def striped8(idx):
    return np.asarray(idx).reshape(8, -1, 16).transpose(0, 2, 1).reshape(128, -1).astype(np.uint16)


def unstriped8(offs):
    return offs.reshape(8, 16, -1).transpose(0, 2, 1).reshape(8, -1).astype(np.int64)


def pick8(x, idx, run):
    r = np.arange(len(x))
    return x[r[:, None], idx[r % (8 * run) // run]]


E2M1 = np.array([0.0, 0.5, 1.0, 1.5, 2.0, 3.0, 4.0, 6.0, -0.0, -0.5, -1.0, -1.5, -2.0, -3.0, -4.0, -6.0])


def pack_weight(w, fmt):
    k, n = w.shape
    w = f64(np.asarray(w, np.float32).astype(ml_dtypes.bfloat16)).reshape(k // 32, 32, n)
    amax = np.abs(w).max(1)
    if fmt == "e4m3":
        byte = np.frexp(amax)[1] - 1 + 127 - 7
    else:
        mant, ex = np.frexp(amax / 6.0)
        byte = np.where(mant > 0.5, ex, ex - 1) + 127
    byte = np.clip(np.where(amax > 0, byte, 1), 1, 254)
    scaled = (w * np.exp2(127.0 - byte)[:, None, :]).reshape(k, n).astype(np.float32)
    by_word = np.ascontiguousarray(scaled.reshape(k // 512, 128, 4, n).transpose(0, 1, 3, 2))
    if fmt == "e4m3":
        words = by_word.astype(ml_dtypes.float8_e4m3fn).view(np.uint8)
    else:
        c = by_word.astype(ml_dtypes.float4_e2m1fn).view(np.uint8) & 0xF
        words = (c[..., 0::2] | (c[..., 1::2] << 4)).reshape(k // 512, 128, 2 * n)
    return np.ascontiguousarray(words), np.ascontiguousarray(byte.astype(np.uint8).reshape(k // 512, 16, n))


def unpack_weight(words, scales, fmt):
    g, _, n = scales.shape
    words = np.ascontiguousarray(words).reshape(g, 128, n, -1)
    if fmt == "e4m3":
        vals = words.view(ml_dtypes.float8_e4m3fn).astype(np.float64)
    else:
        nib = np.empty((g, 128, n, 4), np.uint8)
        nib[..., 0::2] = words & 0xF
        nib[..., 1::2] = words >> 4
        vals = E2M1[nib]
    vals = vals * np.repeat(np.exp2(scales.astype(np.float64) - 127.0), 8, axis=1)[..., None]
    return vals.transpose(0, 1, 3, 2).reshape(g * 512, n)


def bf(x):
    return np.asarray(x, np.float32).astype(ml_dtypes.bfloat16)


def planes(Y):
    r, m = Y.shape
    b = f64(bf(Y)).reshape(r // 32, 32, m)
    amax = np.abs(b).max(1)
    byte = np.clip(np.where(amax > 0, np.frexp(amax)[1] - 1 + 127 - 7, 1), 1, 254)
    codes = (b * np.exp2(127.0 - byte)[:, None, :]).reshape(r, m).astype(np.float32).astype(ml_dtypes.float8_e4m3fn).view(np.uint8)
    words = codes.reshape(r // 512, 128, 4, m).transpose(0, 1, 3, 2)
    return np.ascontiguousarray(words), np.ascontiguousarray(byte.astype(np.uint8).reshape(r // 512, 16, m))


K, T, J, L, V, N = 1024, 2048, 512, 512, 512, 512


def setup_inputs():
    n = np.random.standard_normal
    idx = np.random.permutation(T)[:J]
    idx2 = np.stack([np.random.randint(0, V, J) for _ in range(8)])
    fk = mx_kscale(K)
    fl = mx_kscale(L)
    xtp = pack_weight(n((K, T)) / fk[:, None], "e2m1")
    wp = pack_weight(n((K, N)) * 1 / np.sqrt(K) * fk[:, None], "e4m3")
    wcp = pack_weight(n((L, N)) * 1 / np.sqrt(L) * fl[:, None], "e2m1")
    return {
        "xt_words": xtp[0],
        "xt_scales": xtp[1],
        "w_words": wp[0],
        "w_scales": wp[1],
        "cd": (n((L, V)) / fl[:, None]).astype(np.float32),
        "wc_words": wcp[0],
        "wc_scales": wcp[1],
        "offs": striped(idx),
        "offs2": striped8(idx2),
    }


def reference(xt_words, xt_scales, w_words, w_scales, cd, wc_words, wc_scales, offs, offs2):
    idx = unstriped(offs)
    idx2 = unstriped8(offs2)
    xtu = unpack_weight(xt_words, xt_scales, "e2m1")
    wu = unpack_weight(w_words, w_scales, "e4m3")
    wcu = unpack_weight(wc_words, wc_scales, "e2m1")
    xtidxg = xtu[:, idx]
    p = wu.T @ xtidxg
    cdq = mxq(f64(cd), 0, "e4m3")
    e = wcu.T @ cdq
    y = np.maximum(p + pick8(e, idx2, 64), 0.0)
    words, scales = planes(y)
    return y, words, scales

@@ -1,0 +1,150 @@
+from contextlib import ExitStack
+
+import concourse.mybir as mybir
+
+K, T, J, L, V, N = 1024, 2048, 512, 512, 512, 512
+FLOPS = 2 * N * J * K + 2 * N * V * L
+
+F32 = mybir.dt.float32
+BF16 = mybir.dt.bfloat16
+I32 = mybir.dt.int32
+U32 = mybir.dt.uint32
+U16 = mybir.dt.uint16
+U8 = mybir.dt.uint8
+FP8X4 = mybir.dt.float8_e4m3fn_x4
+FP4X4 = mybir.dt.float4_e2m1fn_x4
+ACT = mybir.ActivationFunctionType
+ALU = mybir.AluOpType
+
+P = 128
+HALF = 256
+
+
+def tile_list_head_tables_pl_kernel(tc, xt_words, xt_scales, w_words, w_scales, cd, wc_words, wc_scales,
+                                        offs, offs2, out_0, out_1, out_2):
+    nc = tc.nc
+    with ExitStack() as ctx:
+        sb = ctx.enter_context(tc.tile_pool(name="sb", bufs=1))
+        ps = ctx.enter_context(tc.psum_pool(name="ps", bufs=1))
+
+        def tile(shape, dtype, name, tag=""):
+            return sb.tile(shape, dtype, name=name, tag=tag, align_bytes=64)
+
+        idx = tile([P, J // 16], U16, "idx")
+        idx2 = tile([P, J // 16], U16, "idx2")
+        xs_raw = tile([P, 2 * T], U8, "xs_raw")
+        wcs_raw = tile([P, N], U8, "wcs_raw")
+        ws_raw = tile([P, 2 * N], U8, "ws_raw")
+        cd_raw = [tile([P, 4, HALF], F32, f"cd_raw{h}", f"codes{h}") for h in range(2)]
+        wc_raw = tile([P, N], U16, "wc_raw")
+        xw_raw = [tile([P, T], U16, f"xw_raw{z}") for z in range(2)]
+        w_raw = tile([P, 2, N], U32, "w_raw")
+
+        nc.gpsimd.memset(wcs_raw[:].bitcast(I32), 0)
+        nc.vector.memset(xs_raw[:].bitcast(I32), 0)
+        nc.gpsimd.memset(ws_raw[:].bitcast(I32), 0)
+
+        def load_scales(dst, src):
+            for q in range(4):
+                nc.sync.dma_start(dst[32 * q: 32 * q + 4, :].rearrange("p (z n) -> p z n", z=src.shape[0]).bitcast(I32),
+                                  src[:, 4 * q: 4 * q + 4, :].rearrange("z r n -> r z n").bitcast(I32))
+
+        cd_rows = cd.rearrange("(p i) v -> p i v", i=4)
+        nc.sync.dma_start(idx[:], offs)
+        nc.sync.dma_start(idx2[:], offs2)
+        nc.sync.dma_start(cd_raw[0][:], cd_rows[:, :, 0:HALF])
+        nc.sync.dma_start(cd_raw[1][:], cd_rows[:, :, HALF:V])
+        nc.sync.dma_start(wc_raw[:].bitcast(I32), wc_words[0].bitcast(I32))
+        load_scales(wcs_raw, wc_scales)
+        nc.sync.dma_start(xw_raw[0][:].bitcast(I32), xt_words[0].bitcast(I32))
+        nc.sync.dma_start(w_raw[:].bitcast(I32), w_words.rearrange("z p n r -> p z (n r)").bitcast(I32))
+        load_scales(xs_raw, xt_scales)
+        nc.sync.dma_start(xw_raw[1][:].bitcast(I32), xt_words[1].bitcast(I32))
+        load_scales(ws_raw, w_scales)
+
+        wcs = tile([P, N], U8, "wcs")
+        cd_bf = [tile([P, HALF, 4], BF16, f"cd_bf{h}", f"rounded{h}") for h in range(2)]
+        cd_codes = tile([P, V], U32, "cd_codes")
+        cd_scales = tile([P, V], U8, "cd_scales")
+        e_ps = [ps.tile([P, V], F32, name=f"e_ps{t}") for t in range(4)]
+
+        def dealt_out(ap):
+            return ap.rearrange("p (t c i) -> p c t i", t=4, i=4)
+
+        def dealt_in(ap):
+            return ap.rearrange("p (c i t) -> p c t i", t=4, i=4)
+
+        def woven_out(ap):
+            return ap.rearrange("p (c i) t -> p c t i", i=4)
+
+        def woven_in(ap):
+            return ap.rearrange("p t (c i) -> p c t i", i=4)
+
+        for h in range(2):
+            nc.vector.tensor_copy(woven_out(cd_bf[h][:]), woven_in(cd_raw[h][:]))
+            if h == 1:
+                wc = tile([P, N], U16, "wc")
+                nc.scalar.copy(dealt_out(wc[:]), dealt_in(wc_raw[:]))
+                nc.gpsimd.tensor_copy(dealt_out(wcs[:]), dealt_in(wcs_raw[:]))
+            nc.vector.quantize_mx(out=cd_codes[:, h * HALF: (h + 1) * HALF].bitcast(FP8X4), scales=cd_scales[:, h * HALF: (h + 1) * HALF],
+                                  in_=cd_bf[h][:].rearrange("p c i -> p (c i)"))
+        for t in range(4):
+            nc.tensor.matmul_mx(out=e_ps[t][:], lhsT=wc[:, t * P: (t + 1) * P].bitcast(FP4X4),
+                                lhsT_scale=wcs[:, t * P: (t + 1) * P],
+                                rhs=cd_codes[:].bitcast(FP8X4), rhs_scale=cd_scales[:], start=True, stop=True)
+
+        cols = HALF // 16
+        xw = tile([P, 2, J], U16, "xw", "rounded1")
+        w = tile([P, 2, N], U32, "w", "rounded0")
+        ws = tile([P, 2 * N], U8, "ws")
+        nc.vector.tensor_copy(xw[:, 0, :], xw_raw[0][:].indirect(idx[:]))
+        xs = tile([P, 2, J], U8, "xs", "codes1")
+        for z in range(2):
+            nc.vector.tensor_copy(xs[:, z, :], xs_raw[:, z * T: (z + 1) * T].indirect(idx[:]))
+        nc.vector.tensor_copy(w[:].rearrange("p z (t c i) -> p z c t i", t=4, i=4),
+                              w_raw[:].rearrange("p z (c i t) -> p z c t i", t=4, i=4))
+        for z in range(2):
+            nc.gpsimd.tensor_copy(dealt_out(ws[:, z * N: (z + 1) * N]), dealt_in(ws_raw[:, z * N: (z + 1) * N]))
+        for h in range(2):
+            nc.vector.tensor_copy(xw[:, 1, h * HALF: (h + 1) * HALF],
+                                  xw_raw[1][:].indirect(idx[:, h * cols: (h + 1) * cols]))
+        p_ps = [[ps.tile([P, 2, HALF], F32, name=f"p_ps{h}{u}") for u in range(2)] for h in range(2)]
+        for h in range(2):
+            slots = slice(h * HALF, (h + 1) * HALF)
+            for z in range(2):
+                for t in range(4):
+                    nc.tensor.matmul_mx(out=p_ps[h][t // 2][:, t % 2, :],
+                                        lhsT=w[:, z, t * P: (t + 1) * P].bitcast(FP8X4),
+                                        lhsT_scale=ws[:, z * N + t * P: z * N + (t + 1) * P],
+                                        rhs=xw[:, z, slots].bitcast(FP4X4), rhs_scale=xs[:, z, slots],
+                                        start=(z == 0 and t % 2 == 0), stop=(z == 1 and t % 2 == 1))
+
+        e = [tile([P, V], F32, f"e{t}") for t in range(4)]
+        g = [tile([P, 4, HALF], F32, f"g{h}") for h in range(2)]
+        for t in range(4):
+            nc.scalar.activation(e[t][:], e_ps[t][:], ACT.Copy)
+            nc.scalar.activation(g[0][:, t, :], e[t][:].indirect(idx2[:, 0:cols]), ACT.Copy)
+        for t in range(4):
+            nc.scalar.activation(g[1][:, t, :], e[t][:].indirect(idx2[:, cols: 2 * cols]), ACT.Copy)
+
+        y_codes = tile([P, J], U32, "y_codes")
+        y_scales = tile([P, J], U8, "y_scales")
+        y_rows = out_0.rearrange("(p t) j -> p t j", t=4)
+        words_out = out_1[0].rearrange("p j r -> p (j r)").bitcast(I32)
+        for h in range(2):
+            slots = slice(h * HALF, (h + 1) * HALF)
+            total = tile([P, 4, HALF], F32, f"total{h}")
+            y = tile([P, 4, HALF], F32, f"y{h}")
+            y_bf = tile([P, HALF, 4], BF16, f"y_bf{h}")
+            for u in range(2):
+                pair = slice(2 * u, 2 * u + 2)
+                nc.vector.tensor_tensor(total[:, pair, :], p_ps[h][u][:], g[h][:, pair, :], ALU.add)
+                nc.scalar.activation(y[:, pair, :], total[:, pair, :], ACT.Relu)
+                nc.sync.dma_start(y_rows[:, pair, slots], y[:, pair, :])
+            nc.vector.tensor_scalar_max(woven_out(y_bf[:]), woven_in(total[:]), 0.0)
+            nc.vector.quantize_mx(out=y_codes[:, slots].bitcast(FP8X4), scales=y_scales[:, slots],
+                                  in_=y_bf[:].rearrange("p c i -> p (c i)"))
+            nc.sync.dma_start(words_out[:, slots], y_codes[:, slots].bitcast(I32))
+        for q in range(4):
+            queue = nc.sync if q % 2 == 0 else nc.scalar
+            queue.dma_start(out_2[0, 4 * q: 4 * q + 4, :].bitcast(I32), y_scales[32 * q: 32 * q + 4, :].bitcast(I32))

@@ -18,6 +18,23 @@ ALU = mybir.AluOpType
 
 P = 128
 HALF = 256
+SCALAR_CAST = 160
+
+
+def dealt_out(ap, run):
+    return ap.rearrange("p (z t c i) -> p z c t i", t=4, i=run, c=P // run)
+
+
+def dealt_in(ap, run):
+    return ap.rearrange("p (z c i t) -> p z c t i", t=4, i=run, c=P // run)
+
+
+def woven_out(ap):
+    return ap.rearrange("p (c i) t -> p c t i", i=4)
+
+
+def woven_in(ap):
+    return ap.rearrange("p t (c i) -> p c t i", i=4)
 
 
 def tile_list_head_tables_pl_kernel(tc, xt_words, xt_scales, w_words, w_scales, cd, wc_words, wc_scales,
@@ -32,61 +49,70 @@ def tile_list_head_tables_pl_kernel(tc, xt_words, xt_scales, w_words, w_scales, 
 
         idx = tile([P, J // 16], U16, "idx")
         idx2 = tile([P, J // 16], U16, "idx2")
-        xs_raw = tile([P, 2 * T], U8, "xs_raw")
+        xs_raw = tile([P, T], U8, "xs_raw")
+        xs = tile([P, 2 * J], U8, "xs")
         wcs_raw = tile([P, N], U8, "wcs_raw")
         ws_raw = tile([P, 2 * N], U8, "ws_raw")
-        cd_raw = [tile([P, 4, HALF], F32, f"cd_raw{h}", f"codes{h}") for h in range(2)]
+        cd_raw = [tile([P, 2, V], F32, f"cd_raw{a}", f"codes{a}") for a in range(2)]
         wc_raw = tile([P, N], U16, "wc_raw")
-        xw_raw = [tile([P, T], U16, f"xw_raw{z}") for z in range(2)]
-        w_raw = tile([P, 2, N], U32, "w_raw")
+        xw_raw = [tile([P, T], U16, f"xw_raw{z}", f"tokens{z}") for z in range(2)]
+        w_raw = tile([P, 2 * N], U32, "w_raw", "weights")
 
-        nc.gpsimd.memset(wcs_raw[:].bitcast(I32), 0)
         nc.vector.memset(xs_raw[:].bitcast(I32), 0)
         nc.gpsimd.memset(ws_raw[:].bitcast(I32), 0)
+        nc.vector.memset(wcs_raw[:].bitcast(I32), 0)
+        nc.vector.memset(xs[:].bitcast(I32), 0)
 
-        def load_scales(dst, src):
+        def load_scales(queue, dst, src):
             for q in range(4):
-                nc.sync.dma_start(dst[32 * q: 32 * q + 4, :].rearrange("p (z n) -> p z n", z=src.shape[0]).bitcast(I32),
-                                  src[:, 4 * q: 4 * q + 4, :].rearrange("z r n -> r z n").bitcast(I32))
+                queue.dma_start(dst[32 * q: 32 * q + 4, :].rearrange("p (z n) -> p z n", z=src.shape[0]).bitcast(I32),
+                                src[:, 4 * q: 4 * q + 4, :].rearrange("z r n -> r z n").bitcast(I32))
 
-        cd_rows = cd.rearrange("(p i) v -> p i v", i=4)
         nc.sync.dma_start(idx[:], offs)
         nc.sync.dma_start(idx2[:], offs2)
-        nc.sync.dma_start(cd_raw[0][:], cd_rows[:, :, 0:HALF])
-        nc.sync.dma_start(cd_raw[1][:], cd_rows[:, :, HALF:V])
+        cd_rows = cd.rearrange("(p i) v -> p i v", i=4)
+        nc.sync.dma_start(cd_raw[0][:], cd_rows[:, 0:2, :])
+        nc.sync.dma_start(xs_raw[0:P:4, :].bitcast(I32), xt_scales.rearrange("z q t -> (z q) t").bitcast(I32))
+        nc.sync.dma_start(cd_raw[1][:], cd_rows[:, 2:4, :])
         nc.sync.dma_start(wc_raw[:].bitcast(I32), wc_words[0].bitcast(I32))
-        load_scales(wcs_raw, wc_scales)
+        load_scales(nc.sync, wcs_raw, wc_scales)
         nc.sync.dma_start(xw_raw[0][:].bitcast(I32), xt_words[0].bitcast(I32))
-        nc.sync.dma_start(w_raw[:].bitcast(I32), w_words.rearrange("z p n r -> p z (n r)").bitcast(I32))
-        load_scales(xs_raw, xt_scales)
-        nc.sync.dma_start(xw_raw[1][:].bitcast(I32), xt_words[1].bitcast(I32))
-        load_scales(ws_raw, w_scales)
+        nc.sync.dma_start(w_raw[:].rearrange("p (z n) -> p z n", z=2).bitcast(I32),
+                          w_words.rearrange("z p n r -> p z (n r)").bitcast(I32))
+        load_scales(nc.gpsimd, ws_raw, w_scales)
 
+        xs_picked = tile([P, J], U8, "xs_picked")
+        nc.vector.tensor_copy(xs_picked[:], xs_raw[:].indirect(idx[:]))
+
+        def move_scales(z):
+            for q in range(4):
+                first = 4 * (16 * z + 4 * q)
+                nc.sync.dma_start(xs[32 * q: 32 * q + 4, z * J: (z + 1) * J].bitcast(I32),
+                                  xs_picked[first: first + 13: 4, :].bitcast(I32))
+
+        move_scales(0)
+        nc.sync.dma_start(xw_raw[1][:].bitcast(I32), xt_words[1].bitcast(I32))
+
+        move_scales(1)
+
+        wc = tile([P, N], U16, "wc", "codes0")
         wcs = tile([P, N], U8, "wcs")
         cd_bf = [tile([P, HALF, 4], BF16, f"cd_bf{h}", f"rounded{h}") for h in range(2)]
         cd_codes = tile([P, V], U32, "cd_codes")
         cd_scales = tile([P, V], U8, "cd_scales")
         e_ps = [ps.tile([P, V], F32, name=f"e_ps{t}") for t in range(4)]
 
-        def dealt_out(ap):
-            return ap.rearrange("p (t c i) -> p c t i", t=4, i=4)
-
-        def dealt_in(ap):
-            return ap.rearrange("p (c i t) -> p c t i", t=4, i=4)
-
-        def woven_out(ap):
-            return ap.rearrange("p (c i) t -> p c t i", i=4)
-
-        def woven_in(ap):
-            return ap.rearrange("p t (c i) -> p c t i", i=4)
-
+        own = HALF - SCALAR_CAST
         for h in range(2):
-            nc.vector.tensor_copy(woven_out(cd_bf[h][:]), woven_in(cd_raw[h][:]))
-            if h == 1:
-                wc = tile([P, N], U16, "wc")
-                nc.scalar.copy(dealt_out(wc[:]), dealt_in(wc_raw[:]))
-                nc.gpsimd.tensor_copy(dealt_out(wcs[:]), dealt_in(wcs_raw[:]))
-            nc.vector.quantize_mx(out=cd_codes[:, h * HALF: (h + 1) * HALF].bitcast(FP8X4), scales=cd_scales[:, h * HALF: (h + 1) * HALF],
+            nc.scalar.activation(cd_bf[h][:, :, 0:2], cd_raw[0][:, :, h * HALF: (h + 1) * HALF].rearrange("p i v -> p v i"), ACT.Copy)
+        nc.scalar.activation(cd_bf[1][:, own:, 2:4], cd_raw[1][:, :, HALF + own:].rearrange("p i v -> p v i"), ACT.Copy)
+        nc.vector.tensor_copy(cd_bf[0][:, :, 2:4], cd_raw[1][:, :, :HALF].rearrange("p i v -> p v i"))
+        nc.vector.tensor_copy(cd_bf[1][:, :own, 2:4], cd_raw[1][:, :, HALF: HALF + own].rearrange("p i v -> p v i"))
+        nc.scalar.copy(dealt_out(wc[:], 8), dealt_in(wc_raw[:], 8))
+        nc.vector.tensor_copy(dealt_out(wcs[:], 16), dealt_in(wcs_raw[:], 16))
+        for h in range(2):
+            codes = slice(h * HALF, (h + 1) * HALF)
+            nc.vector.quantize_mx(out=cd_codes[:, codes].bitcast(FP8X4), scales=cd_scales[:, codes],
                                   in_=cd_bf[h][:].rearrange("p c i -> p (c i)"))
         for t in range(4):
             nc.tensor.matmul_mx(out=e_ps[t][:], lhsT=wc[:, t * P: (t + 1) * P].bitcast(FP4X4),
@@ -94,35 +120,31 @@ def tile_list_head_tables_pl_kernel(tc, xt_words, xt_scales, w_words, w_scales, 
                                 rhs=cd_codes[:].bitcast(FP8X4), rhs_scale=cd_scales[:], start=True, stop=True)
 
         cols = HALF // 16
+        e = [tile([P, V], F32, f"e{t}") for t in range(4)]
         xw = tile([P, 2, J], U16, "xw", "rounded1")
-        w = tile([P, 2, N], U32, "w", "rounded0")
-        ws = tile([P, 2 * N], U8, "ws")
         nc.vector.tensor_copy(xw[:, 0, :], xw_raw[0][:].indirect(idx[:]))
-        xs = tile([P, 2, J], U8, "xs", "codes1")
-        for z in range(2):
-            nc.vector.tensor_copy(xs[:, z, :], xs_raw[:, z * T: (z + 1) * T].indirect(idx[:]))
-        nc.vector.tensor_copy(w[:].rearrange("p z (t c i) -> p z c t i", t=4, i=4),
-                              w_raw[:].rearrange("p z (c i t) -> p z c t i", t=4, i=4))
-        for z in range(2):
-            nc.gpsimd.tensor_copy(dealt_out(ws[:, z * N: (z + 1) * N]), dealt_in(ws_raw[:, z * N: (z + 1) * N]))
+        w = tile([P, 2 * N], U32, "w", "tokens0")
+        nc.vector.tensor_copy(dealt_out(w[:], 4), dealt_in(w_raw[:], 4))
+        ws = tile([P, 2 * N], U8, "ws", "weights")
+        nc.vector.tensor_copy(dealt_out(ws[:], 16), dealt_in(ws_raw[:], 16))
+        nc.vector.tensor_copy(e[3][:], e_ps[3][:])
         for h in range(2):
             nc.vector.tensor_copy(xw[:, 1, h * HALF: (h + 1) * HALF],
                                   xw_raw[1][:].indirect(idx[:, h * cols: (h + 1) * cols]))
         p_ps = [[ps.tile([P, 2, HALF], F32, name=f"p_ps{h}{u}") for u in range(2)] for h in range(2)]
-        for h in range(2):
-            slots = slice(h * HALF, (h + 1) * HALF)
-            for z in range(2):
-                for t in range(4):
-                    nc.tensor.matmul_mx(out=p_ps[h][t // 2][:, t % 2, :],
-                                        lhsT=w[:, z, t * P: (t + 1) * P].bitcast(FP8X4),
-                                        lhsT_scale=ws[:, z * N + t * P: z * N + (t + 1) * P],
-                                        rhs=xw[:, z, slots].bitcast(FP4X4), rhs_scale=xs[:, z, slots],
-                                        start=(z == 0 and t % 2 == 0), stop=(z == 1 and t % 2 == 1))
+        for z, h in ((0, 0), (0, 1), (1, 0), (1, 1)):
+            for t in range(4):
+                features = slice(z * N + t * P, z * N + (t + 1) * P)
+                nc.tensor.matmul_mx(out=p_ps[h][t // 2][:, t % 2, :],
+                                    lhsT=w[:, features].bitcast(FP8X4), lhsT_scale=ws[:, features],
+                                    rhs=xw[:, z, h * HALF: (h + 1) * HALF].bitcast(FP4X4),
+                                    rhs_scale=xs[:, z * J + h * HALF: z * J + (h + 1) * HALF],
+                                    start=(z == 0 and t % 2 == 0), stop=(z == 1 and t % 2 == 1))
 
-        e = [tile([P, V], F32, f"e{t}") for t in range(4)]
         g = [tile([P, 4, HALF], F32, f"g{h}") for h in range(2)]
         for t in range(4):
-            nc.scalar.activation(e[t][:], e_ps[t][:], ACT.Copy)
+            if t < 3:
+                nc.scalar.activation(e[t][:], e_ps[t][:], ACT.Copy)
             nc.scalar.activation(g[0][:, t, :], e[t][:].indirect(idx2[:, 0:cols]), ACT.Copy)
         for t in range(4):
             nc.scalar.activation(g[1][:, t, :], e[t][:].indirect(idx2[:, cols: 2 * cols]), ACT.Copy)
@@ -133,9 +155,9 @@ def tile_list_head_tables_pl_kernel(tc, xt_words, xt_scales, w_words, w_scales, 
         words_out = out_1[0].rearrange("p j r -> p (j r)").bitcast(I32)
         for h in range(2):
             slots = slice(h * HALF, (h + 1) * HALF)
-            total = tile([P, 4, HALF], F32, f"total{h}")
+            total = tile([P, 4, HALF], F32, f"total{h}", "")
             y = tile([P, 4, HALF], F32, f"y{h}")
-            y_bf = tile([P, HALF, 4], BF16, f"y_bf{h}")
+            y_bf = tile([P, HALF, 4], BF16, f"y_bf{h}", f"woven{h}")
             for u in range(2):
                 pair = slice(2 * u, 2 * u + 2)
                 nc.vector.tensor_tensor(total[:, pair, :], p_ps[h][u][:], g[h][:, pair, :], ALU.add)

@@ -1,3 +1,4 @@
+import itertools
 from contextlib import ExitStack
 
 import concourse.mybir as mybir
@@ -18,7 +19,7 @@ ALU = mybir.AluOpType
 
 P = 128
 HALF = 256
-SCALAR_CAST = 160
+SCALAR_CAST = 80
 
 
 def dealt_out(ap, run):
@@ -53,86 +54,83 @@ def tile_list_head_tables_pl_kernel(tc, xt_words, xt_scales, w_words, w_scales, 
         xs = tile([P, 2 * J], U8, "xs")
         wcs_raw = tile([P, N], U8, "wcs_raw")
         ws_raw = tile([P, 2 * N], U8, "ws_raw")
-        cd_raw = [tile([P, 2, V], F32, f"cd_raw{a}", f"codes{a}") for a in range(2)]
+        cd_raw = [tile([P, 4, HALF], F32, f"cd_raw{h}", f"codes{h}") for h in range(2)]
         wc_raw = tile([P, N], U16, "wc_raw")
         xw_raw = [tile([P, T], U16, f"xw_raw{z}", f"tokens{z}") for z in range(2)]
         w_raw = tile([P, 2 * N], U32, "w_raw", "weights")
 
-        nc.vector.memset(xs_raw[:].bitcast(I32), 0)
-        nc.gpsimd.memset(ws_raw[:].bitcast(I32), 0)
+        nc.gpsimd.memset(xs_raw[:, :T // 2].bitcast(I32), 0)
+        nc.vector.memset(xs_raw[:, T // 2:].bitcast(I32), 0)
         nc.vector.memset(wcs_raw[:].bitcast(I32), 0)
-        nc.vector.memset(xs[:].bitcast(I32), 0)
+        nc.gpsimd.memset(ws_raw[:].bitcast(I32), 0)
+        nc.gpsimd.memset(xs[:].bitcast(I32), 0)
 
         def load_scales(queue, dst, src):
             for q in range(4):
                 queue.dma_start(dst[32 * q: 32 * q + 4, :].rearrange("p (z n) -> p z n", z=src.shape[0]).bitcast(I32),
                                 src[:, 4 * q: 4 * q + 4, :].rearrange("z r n -> r z n").bitcast(I32))
 
-        nc.sync.dma_start(idx[:], offs)
-        nc.sync.dma_start(idx2[:], offs2)
         cd_rows = cd.rearrange("(p i) v -> p i v", i=4)
-        nc.sync.dma_start(cd_raw[0][:], cd_rows[:, 0:2, :])
+        nc.sync.dma_start(idx[:], offs)
+        nc.sync.dma_start(cd_raw[0][:], cd_rows[:, :, :HALF])
         nc.sync.dma_start(xs_raw[0:P:4, :].bitcast(I32), xt_scales.rearrange("z q t -> (z q) t").bitcast(I32))
-        nc.sync.dma_start(cd_raw[1][:], cd_rows[:, 2:4, :])
+        nc.sync.dma_start(cd_raw[1][:], cd_rows[:, :, HALF:])
         nc.sync.dma_start(wc_raw[:].bitcast(I32), wc_words[0].bitcast(I32))
         load_scales(nc.sync, wcs_raw, wc_scales)
         nc.sync.dma_start(xw_raw[0][:].bitcast(I32), xt_words[0].bitcast(I32))
         nc.sync.dma_start(w_raw[:].rearrange("p (z n) -> p z n", z=2).bitcast(I32),
                           w_words.rearrange("z p n r -> p z (n r)").bitcast(I32))
-        load_scales(nc.gpsimd, ws_raw, w_scales)
+        nc.sync.dma_start(idx2[:], offs2)
+        load_scales(nc.sync, ws_raw, w_scales)
+        nc.sync.dma_start(xw_raw[1][:].bitcast(I32), xt_words[1].bitcast(I32))
 
         xs_picked = tile([P, J], U8, "xs_picked")
         nc.vector.tensor_copy(xs_picked[:], xs_raw[:].indirect(idx[:]))
+        for z, q in itertools.product(range(2), range(4)):
+            first = 4 * (16 * z + 4 * q)
+            queue = nc.gpsimd if (z, q) == (1, 3) else nc.sync
+            queue.dma_start(xs[32 * q: 32 * q + 4, z * J: (z + 1) * J].bitcast(I32),
+                            xs_picked[first: first + 13: 4, :].bitcast(I32))
 
-        def move_scales(z):
-            for q in range(4):
-                first = 4 * (16 * z + 4 * q)
-                nc.sync.dma_start(xs[32 * q: 32 * q + 4, z * J: (z + 1) * J].bitcast(I32),
-                                  xs_picked[first: first + 13: 4, :].bitcast(I32))
-
-        move_scales(0)
-        nc.sync.dma_start(xw_raw[1][:].bitcast(I32), xt_words[1].bitcast(I32))
-
-        move_scales(1)
-
-        wc = tile([P, N], U16, "wc", "codes0")
         wcs = tile([P, N], U8, "wcs")
         cd_bf = [tile([P, HALF, 4], BF16, f"cd_bf{h}", f"rounded{h}") for h in range(2)]
         cd_codes = tile([P, V], U32, "cd_codes")
         cd_scales = tile([P, V], U8, "cd_scales")
         e_ps = [ps.tile([P, V], F32, name=f"e_ps{t}") for t in range(4)]
 
-        own = HALF - SCALAR_CAST
-        for h in range(2):
-            nc.scalar.activation(cd_bf[h][:, :, 0:2], cd_raw[0][:, :, h * HALF: (h + 1) * HALF].rearrange("p i v -> p v i"), ACT.Copy)
-        nc.scalar.activation(cd_bf[1][:, own:, 2:4], cd_raw[1][:, :, HALF + own:].rearrange("p i v -> p v i"), ACT.Copy)
-        nc.vector.tensor_copy(cd_bf[0][:, :, 2:4], cd_raw[1][:, :, :HALF].rearrange("p i v -> p v i"))
-        nc.vector.tensor_copy(cd_bf[1][:, :own, 2:4], cd_raw[1][:, :, HALF: HALF + own].rearrange("p i v -> p v i"))
-        nc.scalar.copy(dealt_out(wc[:], 8), dealt_in(wc_raw[:], 8))
-        nc.vector.tensor_copy(dealt_out(wcs[:], 16), dealt_in(wcs_raw[:], 16))
-        for h in range(2):
+        def quantize_codes(h):
             codes = slice(h * HALF, (h + 1) * HALF)
             nc.vector.quantize_mx(out=cd_codes[:, codes].bitcast(FP8X4), scales=cd_scales[:, codes],
                                   in_=cd_bf[h][:].rearrange("p c i -> p (c i)"))
+
+        own = HALF - SCALAR_CAST
+        nc.scalar.activation(woven_out(cd_bf[0][:]), woven_in(cd_raw[0][:]), ACT.Copy)
+        nc.scalar.activation(woven_out(cd_bf[1][:, own:, :]), woven_in(cd_raw[1][:, :, own:]), ACT.Copy)
+        wc = tile([P, N], U16, "wc", "codes0")
+        nc.scalar.copy(dealt_out(wc[:], 8), dealt_in(wc_raw[:], 8))
+        nc.vector.tensor_copy(woven_out(cd_bf[1][:, :own, :]), woven_in(cd_raw[1][:, :, :own]))
+        quantize_codes(0)
+        nc.vector.tensor_copy(dealt_out(wcs[:], 16), dealt_in(wcs_raw[:], 16))
+        quantize_codes(1)
         for t in range(4):
             nc.tensor.matmul_mx(out=e_ps[t][:], lhsT=wc[:, t * P: (t + 1) * P].bitcast(FP4X4),
                                 lhsT_scale=wcs[:, t * P: (t + 1) * P],
                                 rhs=cd_codes[:].bitcast(FP8X4), rhs_scale=cd_scales[:], start=True, stop=True)
 
         cols = HALF // 16
-        e = [tile([P, V], F32, f"e{t}") for t in range(4)]
         xw = tile([P, 2, J], U16, "xw", "rounded1")
         nc.vector.tensor_copy(xw[:, 0, :], xw_raw[0][:].indirect(idx[:]))
         w = tile([P, 2 * N], U32, "w", "tokens0")
         nc.vector.tensor_copy(dealt_out(w[:], 4), dealt_in(w_raw[:], 4))
-        ws = tile([P, 2 * N], U8, "ws", "weights")
-        nc.vector.tensor_copy(dealt_out(ws[:], 16), dealt_in(ws_raw[:], 16))
-        nc.vector.tensor_copy(e[3][:], e_ps[3][:])
+        ws = tile([P, 2 * N], U8, "ws")
+        nc.gpsimd.tensor_copy(dealt_out(ws[:], 16), dealt_in(ws_raw[:], 16))
+        e = [tile([P, V], F32, f"e{t}", "weights" if t == 2 else "") for t in range(4)]
+        nc.vector.tensor_copy(e[2][:], e_ps[2][:])
         for h in range(2):
             nc.vector.tensor_copy(xw[:, 1, h * HALF: (h + 1) * HALF],
                                   xw_raw[1][:].indirect(idx[:, h * cols: (h + 1) * cols]))
         p_ps = [[ps.tile([P, 2, HALF], F32, name=f"p_ps{h}{u}") for u in range(2)] for h in range(2)]
-        for z, h in ((0, 0), (0, 1), (1, 0), (1, 1)):
+        for h, z in itertools.product(range(2), repeat=2):
             for t in range(4):
                 features = slice(z * N + t * P, z * N + (t + 1) * P)
                 nc.tensor.matmul_mx(out=p_ps[h][t // 2][:, t % 2, :],
@@ -141,13 +139,20 @@ def tile_list_head_tables_pl_kernel(tc, xt_words, xt_scales, w_words, w_scales, 
                                     rhs_scale=xs[:, z * J + h * HALF: z * J + (h + 1) * HALF],
                                     start=(z == 0 and t % 2 == 0), stop=(z == 1 and t % 2 == 1))
 
-        g = [tile([P, 4, HALF], F32, f"g{h}") for h in range(2)]
+        g = [[tile([P, 2, HALF], F32, f"g{h}{u}", "tokens1" if (h, u) == (0, 1) else "") for u in range(2)]
+             for h in range(2)]
+
+        def picked(h, t):
+            return g[h][t // 2][:, t % 2, :], e[t][:].indirect(idx2[:, h * cols: (h + 1) * cols])
+
+        for t in range(2):
+            nc.scalar.activation(e[t][:], e_ps[t][:], ACT.Copy)
+            nc.scalar.activation(*picked(0, t), ACT.Copy)
+        nc.scalar.activation(e[3][:], e_ps[3][:], ACT.Copy)
+        for t in range(2, 4):
+            nc.vector.tensor_copy(*picked(0, t))
         for t in range(4):
-            if t < 3:
-                nc.scalar.activation(e[t][:], e_ps[t][:], ACT.Copy)
-            nc.scalar.activation(g[0][:, t, :], e[t][:].indirect(idx2[:, 0:cols]), ACT.Copy)
-        for t in range(4):
-            nc.scalar.activation(g[1][:, t, :], e[t][:].indirect(idx2[:, cols: 2 * cols]), ACT.Copy)
+            nc.scalar.activation(*picked(1, t), ACT.Copy)
 
         y_codes = tile([P, J], U32, "y_codes")
         y_scales = tile([P, J], U8, "y_scales")
@@ -160,13 +165,17 @@ def tile_list_head_tables_pl_kernel(tc, xt_words, xt_scales, w_words, w_scales, 
             y_bf = tile([P, HALF, 4], BF16, f"y_bf{h}", f"woven{h}")
             for u in range(2):
                 pair = slice(2 * u, 2 * u + 2)
-                nc.vector.tensor_tensor(total[:, pair, :], p_ps[h][u][:], g[h][:, pair, :], ALU.add)
+                nc.vector.tensor_tensor(total[:, pair, :], p_ps[h][u][:], g[h][u][:], ALU.add)
                 nc.scalar.activation(y[:, pair, :], total[:, pair, :], ACT.Relu)
                 nc.sync.dma_start(y_rows[:, pair, slots], y[:, pair, :])
-            nc.vector.tensor_scalar_max(woven_out(y_bf[:]), woven_in(total[:]), 0.0)
-            nc.vector.quantize_mx(out=y_codes[:, slots].bitcast(FP8X4), scales=y_scales[:, slots],
-                                  in_=y_bf[:].rearrange("p c i -> p (c i)"))
-            nc.sync.dma_start(words_out[:, slots], y_codes[:, slots].bitcast(I32))
+            pieces = [slice(0, HALF)] if h == 0 else [slice(0, P), slice(P, HALF)]
+            for piece in pieces:
+                nc.vector.tensor_scalar_max(woven_out(y_bf[:, piece, :]), woven_in(total[:, :, piece]), 0.0)
+            for piece in pieces:
+                place = slice(h * HALF + piece.start, h * HALF + piece.stop)
+                nc.vector.quantize_mx(out=y_codes[:, place].bitcast(FP8X4), scales=y_scales[:, place],
+                                      in_=y_bf[:, piece, :].rearrange("p c i -> p (c i)"))
+        nc.sync.dma_start(words_out, y_codes[:].bitcast(I32))
         for q in range(4):
             queue = nc.sync if q % 2 == 0 else nc.scalar
             queue.dma_start(out_2[0, 4 * q: 4 * q + 4, :].bitcast(I32), y_scales[32 * q: 32 * q + 4, :].bitcast(I32))

import itertools
from contextlib import ExitStack

import concourse.mybir as mybir

K, T, J, L, V, N = 1024, 2048, 512, 512, 512, 512
FLOPS = 2 * N * J * K + 2 * N * V * L

F32 = mybir.dt.float32
BF16 = mybir.dt.bfloat16
I32 = mybir.dt.int32
U32 = mybir.dt.uint32
U16 = mybir.dt.uint16
U8 = mybir.dt.uint8
FP8X4 = mybir.dt.float8_e4m3fn_x4
FP4X4 = mybir.dt.float4_e2m1fn_x4
ACT = mybir.ActivationFunctionType
ALU = mybir.AluOpType

P = 128
HALF = 256
SCALAR_CAST = 80


def dealt_out(ap, run):
    return ap.rearrange("p (z t c i) -> p z c t i", t=4, i=run, c=P // run)


def dealt_in(ap, run):
    return ap.rearrange("p (z c i t) -> p z c t i", t=4, i=run, c=P // run)


def woven_out(ap):
    return ap.rearrange("p (c i) t -> p c t i", i=4)


def woven_in(ap):
    return ap.rearrange("p t (c i) -> p c t i", i=4)


def tile_list_head_tables_pl_kernel(tc, xt_words, xt_scales, w_words, w_scales, cd, wc_words, wc_scales,
                                        offs, offs2, out_0, out_1, out_2):
    nc = tc.nc
    with ExitStack() as ctx:
        sb = ctx.enter_context(tc.tile_pool(name="sb", bufs=1))
        ps = ctx.enter_context(tc.psum_pool(name="ps", bufs=1))

        def tile(shape, dtype, name, tag=""):
            return sb.tile(shape, dtype, name=name, tag=tag, align_bytes=64)

        idx = tile([P, J // 16], U16, "idx")
        idx2 = tile([P, J // 16], U16, "idx2")
        xs_raw = tile([P, T], U8, "xs_raw")
        xs = tile([P, 2 * J], U8, "xs")
        wcs_raw = tile([P, N], U8, "wcs_raw")
        ws_raw = tile([P, 2 * N], U8, "ws_raw")
        cd_raw = [tile([P, 4, HALF], F32, f"cd_raw{h}", f"codes{h}") for h in range(2)]
        wc_raw = tile([P, N], U16, "wc_raw")
        xw_raw = [tile([P, T], U16, f"xw_raw{z}", f"tokens{z}") for z in range(2)]
        w_raw = tile([P, 2 * N], U32, "w_raw", "weights")

        nc.gpsimd.memset(xs_raw[:, :T // 2].bitcast(I32), 0)
        nc.vector.memset(xs_raw[:, T // 2:].bitcast(I32), 0)
        nc.vector.memset(wcs_raw[:].bitcast(I32), 0)
        nc.gpsimd.memset(ws_raw[:].bitcast(I32), 0)
        nc.gpsimd.memset(xs[:].bitcast(I32), 0)

        def load_scales(queue, dst, src):
            for q in range(4):
                queue.dma_start(dst[32 * q: 32 * q + 4, :].rearrange("p (z n) -> p z n", z=src.shape[0]).bitcast(I32),
                                src[:, 4 * q: 4 * q + 4, :].rearrange("z r n -> r z n").bitcast(I32))

        cd_rows = cd.rearrange("(p i) v -> p i v", i=4)
        nc.sync.dma_start(idx[:], offs)
        nc.sync.dma_start(cd_raw[0][:], cd_rows[:, :, :HALF])
        nc.sync.dma_start(xs_raw[0:P:4, :].bitcast(I32), xt_scales.rearrange("z q t -> (z q) t").bitcast(I32))
        nc.sync.dma_start(cd_raw[1][:], cd_rows[:, :, HALF:])
        nc.sync.dma_start(wc_raw[:].bitcast(I32), wc_words[0].bitcast(I32))
        load_scales(nc.sync, wcs_raw, wc_scales)
        nc.sync.dma_start(xw_raw[0][:].bitcast(I32), xt_words[0].bitcast(I32))
        nc.sync.dma_start(w_raw[:].rearrange("p (z n) -> p z n", z=2).bitcast(I32),
                          w_words.rearrange("z p n r -> p z (n r)").bitcast(I32))
        nc.sync.dma_start(idx2[:], offs2)
        load_scales(nc.sync, ws_raw, w_scales)
        nc.sync.dma_start(xw_raw[1][:].bitcast(I32), xt_words[1].bitcast(I32))

        xs_picked = tile([P, J], U8, "xs_picked")
        nc.vector.tensor_copy(xs_picked[:], xs_raw[:].indirect(idx[:]))
        for z, q in itertools.product(range(2), range(4)):
            first = 4 * (16 * z + 4 * q)
            queue = nc.gpsimd if (z, q) == (1, 3) else nc.sync
            queue.dma_start(xs[32 * q: 32 * q + 4, z * J: (z + 1) * J].bitcast(I32),
                            xs_picked[first: first + 13: 4, :].bitcast(I32))

        wcs = tile([P, N], U8, "wcs")
        cd_bf = [tile([P, HALF, 4], BF16, f"cd_bf{h}", f"rounded{h}") for h in range(2)]
        cd_codes = tile([P, V], U32, "cd_codes")
        cd_scales = tile([P, V], U8, "cd_scales")
        e_ps = [ps.tile([P, V], F32, name=f"e_ps{t}") for t in range(4)]

        def quantize_codes(h):
            codes = slice(h * HALF, (h + 1) * HALF)
            nc.vector.quantize_mx(out=cd_codes[:, codes].bitcast(FP8X4), scales=cd_scales[:, codes],
                                  in_=cd_bf[h][:].rearrange("p c i -> p (c i)"))

        own = HALF - SCALAR_CAST
        nc.scalar.activation(woven_out(cd_bf[0][:]), woven_in(cd_raw[0][:]), ACT.Copy)
        nc.scalar.activation(woven_out(cd_bf[1][:, own:, :]), woven_in(cd_raw[1][:, :, own:]), ACT.Copy)
        wc = tile([P, N], U16, "wc", "codes0")
        nc.scalar.copy(dealt_out(wc[:], 8), dealt_in(wc_raw[:], 8))
        nc.vector.tensor_copy(woven_out(cd_bf[1][:, :own, :]), woven_in(cd_raw[1][:, :, :own]))
        quantize_codes(0)
        nc.vector.tensor_copy(dealt_out(wcs[:], 16), dealt_in(wcs_raw[:], 16))
        quantize_codes(1)
        for t in range(4):
            nc.tensor.matmul_mx(out=e_ps[t][:], lhsT=wc[:, t * P: (t + 1) * P].bitcast(FP4X4),
                                lhsT_scale=wcs[:, t * P: (t + 1) * P],
                                rhs=cd_codes[:].bitcast(FP8X4), rhs_scale=cd_scales[:], start=True, stop=True)

        cols = HALF // 16
        xw = tile([P, 2, J], U16, "xw", "rounded1")
        nc.vector.tensor_copy(xw[:, 0, :], xw_raw[0][:].indirect(idx[:]))
        w = tile([P, 2 * N], U32, "w", "tokens0")
        nc.vector.tensor_copy(dealt_out(w[:], 4), dealt_in(w_raw[:], 4))
        ws = tile([P, 2 * N], U8, "ws")
        nc.gpsimd.tensor_copy(dealt_out(ws[:], 16), dealt_in(ws_raw[:], 16))
        e = [tile([P, V], F32, f"e{t}", "weights" if t == 2 else "") for t in range(4)]
        nc.vector.tensor_copy(e[2][:], e_ps[2][:])
        for h in range(2):
            nc.vector.tensor_copy(xw[:, 1, h * HALF: (h + 1) * HALF],
                                  xw_raw[1][:].indirect(idx[:, h * cols: (h + 1) * cols]))
        p_ps = [[ps.tile([P, 2, HALF], F32, name=f"p_ps{h}{u}") for u in range(2)] for h in range(2)]
        for h, z in itertools.product(range(2), repeat=2):
            for t in range(4):
                features = slice(z * N + t * P, z * N + (t + 1) * P)
                nc.tensor.matmul_mx(out=p_ps[h][t // 2][:, t % 2, :],
                                    lhsT=w[:, features].bitcast(FP8X4), lhsT_scale=ws[:, features],
                                    rhs=xw[:, z, h * HALF: (h + 1) * HALF].bitcast(FP4X4),
                                    rhs_scale=xs[:, z * J + h * HALF: z * J + (h + 1) * HALF],
                                    start=(z == 0 and t % 2 == 0), stop=(z == 1 and t % 2 == 1))

        g = [[tile([P, 2, HALF], F32, f"g{h}{u}", "tokens1" if (h, u) == (0, 1) else "") for u in range(2)]
             for h in range(2)]

        def picked(h, t):
            return g[h][t // 2][:, t % 2, :], e[t][:].indirect(idx2[:, h * cols: (h + 1) * cols])

        for t in range(2):
            nc.scalar.activation(e[t][:], e_ps[t][:], ACT.Copy)
            nc.scalar.activation(*picked(0, t), ACT.Copy)
        nc.scalar.activation(e[3][:], e_ps[3][:], ACT.Copy)
        for t in range(2, 4):
            nc.vector.tensor_copy(*picked(0, t))
        for t in range(4):
            nc.scalar.activation(*picked(1, t), ACT.Copy)

        y_codes = tile([P, J], U32, "y_codes")
        y_scales = tile([P, J], U8, "y_scales")
        y_rows = out_0.rearrange("(p t) j -> p t j", t=4)
        words_out = out_1[0].rearrange("p j r -> p (j r)").bitcast(I32)
        for h in range(2):
            slots = slice(h * HALF, (h + 1) * HALF)
            total = tile([P, 4, HALF], F32, f"total{h}", "")
            y = tile([P, 4, HALF], F32, f"y{h}")
            y_bf = tile([P, HALF, 4], BF16, f"y_bf{h}", f"woven{h}")
            for u in range(2):
                pair = slice(2 * u, 2 * u + 2)
                nc.vector.tensor_tensor(total[:, pair, :], p_ps[h][u][:], g[h][u][:], ALU.add)
                nc.scalar.activation(y[:, pair, :], total[:, pair, :], ACT.Relu)
                nc.sync.dma_start(y_rows[:, pair, slots], y[:, pair, :])
            pieces = [slice(0, HALF)] if h == 0 else [slice(0, P), slice(P, HALF)]
            for piece in pieces:
                nc.vector.tensor_scalar_max(woven_out(y_bf[:, piece, :]), woven_in(total[:, :, piece]), 0.0)
            for piece in pieces:
                place = slice(h * HALF + piece.start, h * HALF + piece.stop)
                nc.vector.quantize_mx(out=y_codes[:, place].bitcast(FP8X4), scales=y_scales[:, place],
                                      in_=y_bf[:, piece, :].rearrange("p c i -> p (c i)"))
        nc.sync.dma_start(words_out, y_codes[:].bitcast(I32))
        for q in range(4):
            queue = nc.sync if q % 2 == 0 else nc.scalar
            queue.dma_start(out_2[0, 4 * q: 4 * q + 4, :].bitcast(I32), y_scales[32 * q: 32 * q + 4, :].bitcast(I32))
